import numpy as np, ml_dtypes
CORES = [36,38,116,118,124,126,164,166,244,246,252,254]
N = 12
GR, GC = 3, 4
L, KA, KB, F = 12, 3, 4, 128
def setup_inputs(rng):
    return {"a": rng.standard_normal((N, 128, KA * 128), dtype=np.float32).astype(ml_dtypes.bfloat16), "b": rng.standard_normal((N, 128, KB * F), dtype=np.float32).astype(ml_dtypes.bfloat16)}
def reference(a, b):
    A, B = a.astype(np.float64), b.astype(np.float64)
    y = np.zeros((N, 128, F))
    for i in range(GR):
        for j in range(GC):
            for k in range(L):
                At = A[i * GC + k // KA][:, 128 * (k % KA):128 * (k % KA) + 128]
                Bt = B[(k // KB) * GC + j][:, F * (k % KB):F * (k % KB) + F]
                y[i * GC + j] += At.T @ Bt
    return {"y": y.astype(ml_dtypes.bfloat16 if a.dtype != np.float64 else np.float64)}

from concourse.bass import DstId, RemoteDMATransfer
from concourse.mybir import AluOpType

GR, GC, KA, KB, TW = 3, 4, 3, 4, 128
WORLD = 256
NLAND, NPIN, NBANK, NCOL, NCALL = 8, 3, 5, 6, 2
MAXB = 0
HELPERS = 0
HELP_LATE = False

SCRATCH = {
    "aa": ("sbuf", [128, 2 * KA * TW], "bfloat16"),
    "bb": ("sbuf", [128, 2 * KB * TW], "bfloat16"),
    "land": ("sbuf", [128, NLAND * TW], "bfloat16"),
    "pb": ("sbuf", [128, (NBANK - 1) * TW], "bfloat16"),
    "pin": ("sbuf", [128, NPIN * TW], "bfloat16"),
    "t0": ("sbuf", [128, TW], "float32"),
    "t1": ("sbuf", [128, TW], "float32"),
    "ysb": ("sbuf", [128, TW], "bfloat16"),
}
for _n in range(NBANK):
    SCRATCH["ps%d" % _n] = ("psum", [128, 512], "float32")
SEMAPHORES = (["ld_a", "ld_b", "yd", "st", "snt"] + ["r%d" % n for n in range(NCOL)] + ["p%d" % n for n in range(NPIN)]
              + ["mm%d" % n for n in range(NBANK)] + ["cp%d" % n for n in range(NCALL)] + ["ad%d" % n for n in range(NPIN)])


def _engines(mask):
    return [e for e in range(16) if (mask >> e) & 1]


def _bits(engines):
    m = 0
    for e in engines:
        m |= 1 << e
    return m


def _runs(ps):
    out = []
    for p in sorted(ps):
        if out and out[-1][0] + out[-1][1] == p:
            out[-1][1] += 1
        else:
            out.append([p, 1])
    return [tuple(x) for x in out]


def _plan(cores, topo):
    def rc(i, j):
        return cores[i * GC + j]

    def place(c):
        return (topo.host(c), topo.chip(c))

    def reach(c):
        return sum(1 for d in cores if d != c and topo.may_write(c, d))

    teams, team_of = {}, {}
    for i in range(GR):
        seen = []
        for j in range(GC):
            p = place(rc(i, j))
            if p not in seen:
                seen.append(p)
            key = (i, seen.index(p))
            teams.setdefault(key, {"cols": [], "cores": []})
            teams[key]["cols"].append(j)
            teams[key]["cores"].append(rc(i, j))
            team_of[rc(i, j)] = key
    mate, member = {}, {}
    for t in teams.values():
        t["by_reach"] = sorted(t["cores"], key=reach)
        for n, c in enumerate(t["cores"]):
            mate[c], member[c] = t["cores"][1 - n], n

    tasks = []
    for (r, J), t in sorted(teams.items()):
        for i in range(GR):
            dests = [rc(i, j) for j in t["cols"]]
            x = [m for m in t["by_reach"] if all(d == m or topo.may_write(m, d) for d in dests)][0]
            ks = list(range(KB * r, KB * r + KB))
            blocked = [k for k in ks if rc(i, k // KA) != x and not topo.may_write(rc(i, k // KA), x)]
            at_dest = blocked if (all(team_of[rc(i, k // KA)] == team_of[dests[0]] for k in blocked)
                                  and len(blocked) <= MAXB) else []
            tasks.append({"x": x, "i": i, "cols": t["cols"], "dests": dests, "ks": ks, "at_dest": at_dest,
                          "late": len(blocked) > len(at_dest), "away": place(dests[0]) != place(x)})
    helpers = []
    for c in cores:
        away = [q for q in tasks if q["x"] == c and q["away"]]
        if len(away) < 2 or not HELPERS:
            continue
        spare = [h for h in range(WORLD) if place(h) == place(c) and h not in cores
                 and all(topo.may_write(h, d) for q in away for d in q["dests"])]
        spare.sort(key=lambda h: topo.die(h) != topo.die(c))
        spare = spare[:HELPERS]
        move = [q for q in away if not q["late"]]
        if HELP_LATE and not move:
            move = away[1:]
        for n, q in enumerate(move):
            q["x"] = spare[n % len(spare)]
            if q["x"] not in helpers:
                helpers.append(q["x"])
    workers = cores + helpers
    site = {}
    for q in tasks:
        for k in q["ks"]:
            for j, d in zip(q["cols"], q["dests"]):
                site[(q["i"], j, k)] = d if k in q["at_dest"] else q["x"]

    need = {}
    for (i, j, k), x in site.items():
        for owner, kind, pos in ((rc(i, k // KA), "A", k % KA), (rc(k // KB, j), "B", k % KB)):
            if owner != x:
                need.setdefault((owner, kind), {}).setdefault(x, set()).add(pos)

    trs = []

    def add(sender, owner, kind, p0, n, dests, depth, dep):
        trs.append({"tid": len(trs), "sender": sender, "owner": owner, "kind": kind, "p0": p0, "n": n, "dests": dests,
                    "depth": depth, "dep": dep, "after": 0})
        return trs[-1]

    for (owner, kind), who in sorted(need.items()):
        m = mate[owner]
        for_mate = set(who.get(m, ()))
        direct, passed = {}, {}
        for x, ps in sorted(who.items()):
            if x == m:
                continue
            book = direct if topo.may_write(owner, x) else passed
            for run in _runs(ps):
                book.setdefault(run, []).append(x)
            if book is passed:
                for_mate |= ps
        if for_mate:
            lo, hi = min(for_mate), max(for_mate)
            direct.setdefault((lo, hi - lo + 1), []).append(m)
        first = None
        for (p0, n), xs in sorted(direct.items()):
            tr = add(owner, owner, kind, p0, n, xs, 1, None)
            if m in xs:
                first = tr
        for (p0, n), xs in sorted(passed.items()):
            add(m, owner, kind, p0, n, xs, 2, first["tid"])

    loc = {c: {} for c in workers}
    nland = {c: 0 for c in workers}
    colors = {c: set() for c in workers}
    per = {"A": KA, "B": KB}
    buf = {"A": "aa", "B": "bb"}
    for c in cores:
        for kind in "AB":
            for p in range(per[kind]):
                loc[c][(c, kind, p)] = (buf[kind], (member[c] * per[kind] + p) * TW, None, 0)
    for tr in trs:
        tr["at"] = {}
        for x in tr["dests"]:
            if x == mate[tr["owner"]]:
                tr["at"][x] = (buf[tr["kind"]], (member[tr["owner"]] * per[tr["kind"]] + tr["p0"]) * TW)
            else:
                tr["at"][x] = ("land", nland[x] * TW)
                nland[x] += tr["n"]
            for p in range(tr["n"]):
                loc[x][(tr["owner"], tr["kind"], tr["p0"] + p)] = (tr["at"][x][0], tr["at"][x][1] + p * TW, tr["tid"], tr["depth"])
        col = 0
        while any(col in colors[x] for x in tr["dests"]):
            col += 1
        tr["sem"] = col
        for x in tr["dests"]:
            colors[x].add(col)

    work = {c: {"groups": [], "calls": []} for c in workers}
    for c in workers:
        groups = {}
        for (i, j, k), x in sorted(site.items()):
            if x != c:
                continue
            la = loc[c][(rc(i, k // KA), "A", k % KA)]
            lb = loc[c][(rc(k // KB, j), "B", k % KB)]
            groups.setdefault(rc(i, j), []).append({"a": la, "b": lb, "depth": max(la[3], lb[3])})
            for l in (la, lb):
                if l[2] is not None and rc(i, j) != c:
                    trs[l[2]]["after"] = 1
        gl = [{"dest": d, "prods": ps, "depth": max(p["depth"] for p in ps), "home": d == c} for d, ps in groups.items()]
        gl.sort(key=lambda q: (not q["home"], q["depth"], place(q["dest"]) == place(c), cores.index(q["dest"])))
        if gl and not gl[0]["home"]:
            gl.insert(0, None)
        for b, q in enumerate(gl):
            if q:
                q["bank"] = b
        work[c]["groups"] = [q for q in gl if q]
        calls = {}
        for q in work[c]["groups"]:
            if not q["home"]:
                calls.setdefault((q["depth"], place(q["dest"]) == place(c), team_of[q["dest"]]), []).append(q)
        work[c]["calls"] = [calls[k] for k in sorted(calls)]
    for tr in trs:
        if tr["dep"] is not None:
            first = trs[tr["dep"]]
            first["after"] = max(first["after"], 1 + tr["after"])
    npin = {c: 0 for c in cores}
    for c in workers:
        for call in work[c]["calls"]:
            for q in call:
                q["pin"] = npin[q["dest"]]
                npin[q["dest"]] += 1
                q["share"] = len(call)
    return {"trs": trs, "work": work, "member": member, "place": place, "nland": nland, "npin": npin, "workers": workers}


def rank_program(g, core, T, topo):
    cores = list(T.cores)
    P = _plan(cores, topo)
    if core not in P["workers"]:
        return
    S, trs, place = T.sem, P["trs"], P["place"]
    is_rank = core in cores

    def engine_sets(src):
        off = [topo.mask(src, d) for d in cores if place(src) != place(d) and topo.may_write(src, d)][0]
        on = [topo.mask(src, d) for d in cores if d != src and place(src) == place(d)][0]
        only_on = on & ~off
        return _engines(off), _engines(only_on if only_on else on)

    def pool(src, dst):
        off, on = engine_sets(src)
        return on if place(src) == place(dst) else off

    sent = [0]
    waited = {}

    def wait(q, name, sem, n):
        if waited.get((name, sem)) != n:
            waited[(name, sem)] = n
            q.wait_ge(S[sem], n)

    def arrived(q, name, tid):
        wait(q, name, "r%d" % trs[tid]["sem"], len(pool(trs[tid]["sender"], core)))

    def send(parts):
        out = []
        for src, dsts, sem, engines in parts:
            ids = []
            for d, _ in dsts:
                rid, pid = topo.addr(d, core)
                ids.append(DstId(rid=rid, pnc=pid))
            out.append(RemoteDMATransfer(dst_ids=ids, dma_engine_mask=_bits(engines), remote_sem=sem,
                                         srcs=[src], dsts=[ap for _, ap in dsts], alu_op=0))
            sent[0] += len(engines)
        g.remote_dma_fused(out, local_sem=S.snt)

    if is_rank:
        me = P["member"][core]
        g.sync.dma_start(T.aa[:, me * KA * TW:(me + 1) * KA * TW], T.a[:, :]).then_inc(S.ld_a, 16)
        g.sync.dma_start(T.bb[:, me * KB * TW:(me + 1) * KB * TW], T.b[:, :]).then_inc(S.ld_b, 16)

    items = []
    for tr in trs:
        if tr["sender"] == core:
            ready = (tr["depth"] - 1) + (0.1 if tr["kind"] == "B" else 0.0)
            items.append((ready, -tr["after"], -tr["n"], tr["tid"], "tiles", tr))
    for n, call in enumerate(P["work"][core]["calls"]):
        items.append((call[0]["depth"] + 0.6, 0, 0, n, "sums", call))
    items.sort(key=lambda x: x[:4])
    for it in items:
        parts = []
        if it[4] == "tiles":
            tr = it[5]
            if tr["dep"] is None:
                wait(g, "g", "ld_a" if tr["kind"] == "A" else "ld_b", 16)
            else:
                arrived(g, "g", tr["dep"])
            name, c0 = ("aa", KA) if tr["kind"] == "A" else ("bb", KB)
            c0 = (P["member"][tr["owner"]] * c0 + tr["p0"]) * TW
            for near in (False, True):
                xs = [x for x in tr["dests"] if (place(x) == place(core)) == near]
                if xs:
                    dsts = [(x, T[tr["at"][x][0]][:, tr["at"][x][1]:tr["at"][x][1] + tr["n"] * TW]) for x in xs]
                    parts.append((T[name][:, c0:c0 + tr["n"] * TW], dsts, S["r%d" % tr["sem"]], pool(core, xs[0])))
        else:
            call, n = it[5], it[3]
            wait(g, "g", "cp%d" % n, len(call))
            for m, q in enumerate(call):
                eng = pool(core, q["dest"])
                share = len(eng) // len(call)
                b = q["bank"] - 1
                parts.append((T.pb[:, b * TW:(b + 1) * TW], [(q["dest"], T.pin[:, q["pin"] * TW:(q["pin"] + 1) * TW])],
                              S["p%d" % q["pin"]], eng[m * share:(m + 1) * share]))
        send(parts)

    te, ve = g.tensor, g.vector
    todo = []
    for q in P["work"][core]["groups"]:
        for n, p in enumerate(q["prods"]):
            todo.append((p["depth"], q["home"], q["depth"], q["bank"], n, p, q))
    todo.sort(key=lambda x: x[:5])
    left = {q["bank"]: len(q["prods"]) for q in P["work"][core]["groups"]}
    for _, _, _, bank, _, p, q in todo:
        for l, ld in ((p["a"], "ld_a"), (p["b"], "ld_b")):
            if l[2] is None:
                wait(te, "te", ld, 16)
            else:
                arrived(te, "te", l[2])
        first = left[bank] == len(q["prods"])
        left[bank] -= 1
        mm = te.matmul(T["ps%d" % bank][:, 0:TW], T[p["a"][0]][:, p["a"][1]:p["a"][1] + TW],
                       T[p["b"][0]][:, p["b"][1]:p["b"][1] + TW], first, left[bank] == 0)
        if left[bank] == 0:
            mm.then_inc(S["mm%d" % bank], 1)

    for n, call in enumerate(P["work"][core]["calls"]):
        for q in call:
            b = q["bank"]
            ve.wait_ge(S["mm%d" % b], 1)
            ve.tensor_copy(T.pb[:, (b - 1) * TW:b * TW], T["ps%d" % b][:, 0:TW]).then_inc(S["cp%d" % n], 1)
    if is_rank:
        terms = []
        for c in P["workers"]:
            for q in P["work"][c]["groups"]:
                if q["dest"] != core:
                    continue
                if q["home"]:
                    terms.append((q["depth"], T.ps0[:, 0:TW], "mm0", 1))
                else:
                    terms.append((q["depth"] + 1, T.pin[:, q["pin"] * TW:(q["pin"] + 1) * TW], "p%d" % q["pin"],
                                  len(pool(c, core)) // q["share"]))
        terms.sort(key=lambda x: x[0])
        acc = terms[0][1]
        ve.wait_ge(S[terms[0][2]], terms[0][3])
        if len(terms) == 1:
            ve.tensor_copy(T.ysb[:, :], acc).then_inc(S.yd, 1)
        for n, (_, ap, sem, cnt) in enumerate(terms[1:]):
            last = n == len(terms) - 2
            ve.wait_ge(S[sem], cnt)
            out = T.ysb[:, :] if last else T["t%d" % (n % 2)][:, :]
            ve.tensor_tensor(out, acc, ap, AluOpType.add).then_inc(S.yd if last else S["ad%d" % n], 1)
            if not last:
                ve.wait_ge(S["ad%d" % n], 1)
            acc = out
        g.sync.wait_ge(S.yd, 1)
        g.sync.dma_start(T.y[:, :], T.ysb[:, :]).then_inc(S.st, 16)
        g.sync.wait_ge(S.st, 16)
    g.wait_ge(S.snt, sent[0])
